import numpy as np
import ml_dtypes


def mxq(x, axis, fmt="e4m3"):
    dtype, down = {"e4m3": (ml_dtypes.float8_e4m3fn, 7), "e5m2": (ml_dtypes.float8_e5m2, 14)}[fmt]
    v = np.moveaxis(np.asarray(x, np.float32).astype(ml_dtypes.bfloat16).astype(np.float64), axis, -1)
    blocks = v.reshape(v.shape[:-1] + (-1, 32))
    amax = np.abs(blocks).max(-1, keepdims=True)
    byte = np.maximum(np.where(amax > 0, np.frexp(amax)[1] - 1 + 127, 0) - down, 1)
    scale = np.exp2(byte - 127.0)
    codes = (blocks / scale).astype(np.float32).astype(dtype).astype(np.float64)
    return np.moveaxis((codes * scale).reshape(v.shape), -1, axis)


WIDE = False


def mx_kscale(k):
    if not WIDE:
        return np.ones(k)
    levels = np.array([10, -10, 5, -5, 0])
    if k % 512:
        return np.exp2(np.random.permutation(np.resize(levels, k // 32))).repeat(32)
    a = np.empty((k // 512, 16))
    for p in range(k // 512):
        a[p, :8] = np.random.permutation(np.resize(levels, 8))
        for g in range(8):
            far = levels[np.abs(levels - a[p, g]) >= 10]
            a[p, g + 8] = far[np.random.randint(len(far))]
    return np.exp2(a.ravel()).repeat(32)


def f64(x):
    return np.asarray(x).astype(np.float64)


def striped(idx):
    return np.tile(idx.reshape(-1, 16).T, (8, 1)).astype(np.uint16)


def unstriped(offs):
    return offs[:16].T.reshape(-1).astype(np.int64)


K, T, E, C, N = 512, 512, 2, 256, 256


def by_expert(wq, xq):
    return np.concatenate([wq[e].T @ xq[:, e * C:(e + 1) * C] for e in range(E)], axis=1)


def setup_inputs():
    n = np.random.standard_normal
    s = mx_kscale(K)[:, None]
    return {
        "xT": (n((K, T)) * s).astype(np.float32),
        "w": (n((E, K, N)) / np.sqrt(K) / s[None]).astype(np.float32),
        "gate": np.tile(np.random.uniform(0.2, 1.0, E * C), (N, 1)).astype(np.float32),
        "offs": striped(np.random.permutation(T)[:E * C]),
    }


def reference(xT, w, gate, offs):
    idx = unstriped(offs)
    xq = mxq(f64(xT)[:, idx], 0, "e4m3")
    y = by_expert(mxq(f64(w), 1, "e4m3"), xq)
    out = np.zeros((N, T))
    out[:, idx] = f64(gate) * y
    return out

@@ -1,0 +1,111 @@
+from contextlib import ExitStack
+
+import concourse.mybir as mybir
+
+K, T, E, C, N = 512, 512, 2, 256, 256
+FLOPS = 2 * K * N * E * C
+
+F32 = mybir.dt.float32
+BF16 = mybir.dt.bfloat16
+U32 = mybir.dt.uint32
+U16 = mybir.dt.uint16
+U8 = mybir.dt.uint8
+FP8X4 = mybir.dt.float8_e4m3fn_x4
+MULT = mybir.AluOpType.mult
+
+P = 128
+PACK = 4
+FB = N // P
+LC = C // 16
+
+
+def tile_routed_moe_kernel(tc, xT, w, gate, offs, out):
+    nc = tc.nc
+    with ExitStack() as ctx:
+        keep = ctx.enter_context(tc.tile_pool(name="keep", bufs=1))
+        psum = ctx.enter_context(tc.psum_pool(name="psum", bufs=1))
+
+        offsets = keep.tile([P, E * C // 16], U16, name="offsets")
+        nc.sync.dma_start(offsets[:], offs)
+
+        x_view = xT.rearrange("(p t) n -> p t n", t=PACK)
+        x_raw = keep.tile([P, PACK, T], F32, name="x_raw")
+        for t in range(PACK):
+            nc.sync.dma_start(x_raw[:, t, :], x_view[:, t, :])
+
+        w_raw = []
+        for e in range(E):
+            raw = keep.tile([P, PACK, N], F32, name="w_raw%d" % e)
+            nc.sync.dma_start(raw[:], w[e].rearrange("(p j) n -> p j n", j=PACK))
+            w_raw.append(raw)
+
+        gates = []
+        for f in range(FB):
+            g = keep.tile([P, E * C], F32, name="gate%d" % f)
+            nc.sync.dma_start(g[:], gate[f * P:(f + 1) * P, :])
+            gates.append(g)
+
+        x_grouped = [keep.tile([P, C, PACK], BF16, name="x_grouped%d" % e, align_bytes=64) for e in range(E)]
+        x_codes = [keep.tile([P, C], U32, name="x_codes%d" % e, align_bytes=64) for e in range(E)]
+        x_scales = [keep.tile([P, C], U8, name="x_scales%d" % e, align_bytes=64) for e in range(E)]
+        w_grouped = [keep.tile([P, N, PACK], BF16, name="w_grouped%d" % e, align_bytes=64) for e in range(E)]
+        w_codes = [keep.tile([P, N], U32, name="w_codes%d" % e, align_bytes=64) for e in range(E)]
+        w_scales = [keep.tile([P, N], U8, name="w_scales%d" % e, align_bytes=64) for e in range(E)]
+        acc = [[psum.tile([P, C], F32, name="acc%d_%d" % (e, f)) for f in range(FB)] for e in range(E)]
+        sums = [[keep.tile([P, C], F32, name="sums%d_%d" % (e, f)) for f in range(FB)] for e in range(E)]
+        windows = [keep.tile([P, T], F32, name="window%d" % f) for f in range(FB)]
+
+        def gather(e, t):
+            nc.vector.tensor_copy(x_grouped[e][:, :, t], x_raw[:, t, :].indirect(offsets[:, e * LC:(e + 1) * LC]))
+
+        def group_w(e, lo, hi):
+            nc.scalar.copy(out=w_grouped[e][:, lo:hi, :], in_=w_raw[e][:, :, lo:hi].rearrange("p j n -> p n j"))
+
+        def quant_x(e):
+            nc.vector.quantize_mx(out=x_codes[e][:].bitcast(FP8X4), scales=x_scales[e][:],
+                                  in_=x_grouped[e][:].rearrange("p c t -> p (c t)"))
+
+        def quant_w(e, lo, hi):
+            nc.vector.quantize_mx(out=w_codes[e][:, lo:hi].bitcast(FP8X4), scales=w_scales[e][:, lo:hi],
+                                  in_=w_grouped[e][:, lo:hi, :].rearrange("p n j -> p (n j)"))
+
+        def multiply(e, f):
+            cols = slice(f * P, (f + 1) * P)
+            nc.tensor.matmul_mx(out=acc[e][f][:], lhsT=w_codes[e][:, cols].bitcast(FP8X4),
+                                lhsT_scale=w_scales[e][:, cols], rhs=x_codes[e][:].bitcast(FP8X4),
+                                rhs_scale=x_scales[e][:], start=True, stop=True)
+
+        def empty(e, f):
+            nc.scalar.copy(out=sums[e][f][:], in_=acc[e][f][:])
+
+        def scatter(e, f):
+            nc.vector.tensor_tensor(windows[f][:].indirect(offsets[:, e * LC:(e + 1) * LC]),
+                                    sums[e][f][:], gates[f][:, e * C:(e + 1) * C], MULT)
+
+        for t in range(PACK):
+            gather(0, t)
+        gather(1, 0)
+        quant_x(0)
+        group_w(0, 0, P)
+        quant_w(0, 0, P)
+        multiply(0, 0)
+        group_w(0, P, N)
+        quant_w(0, P, N)
+        multiply(0, 1)
+        empty(0, 0)
+        group_w(1, 0, N)
+        quant_w(1, 0, N)
+        empty(0, 1)
+        for t in range(1, PACK):
+            gather(1, t)
+        scatter(0, 0)
+        quant_x(1)
+        multiply(1, 0)
+        multiply(1, 1)
+        empty(1, 0)
+        empty(1, 1)
+        scatter(0, 1)
+        scatter(1, 0)
+        nc.sync.dma_start(out[0:P, :], windows[0][:])
+        scatter(1, 1)
+        nc.sync.dma_start(out[P:2 * P, :], windows[1][:])

@@ -29,9 +29,12 @@ def tile_routed_moe_kernel(tc, xT, w, gate, offs, out):
         nc.sync.dma_start(offsets[:], offs)
 
         x_view = xT.rearrange("(p t) n -> p t n", t=PACK)
-        x_raw = keep.tile([P, PACK, T], F32, name="x_raw")
+        planes = []
         for t in range(PACK):
-            nc.sync.dma_start(x_raw[:, t, :], x_view[:, t, :])
+            plane = keep.tile([P, T], F32, name="plane%d" % t)
+            nc.sync.dma_start(plane[:], x_view[:, t, :])
+            planes.append(plane)
+        picked = [keep.tile([P, PACK, C], F32, name="picked%d" % e) for e in range(E)]
 
         w_raw = []
         for e in range(E):
@@ -56,7 +59,10 @@ def tile_routed_moe_kernel(tc, xT, w, gate, offs, out):
         windows = [keep.tile([P, T], F32, name="window%d" % f) for f in range(FB)]
 
         def gather(e, t):
-            nc.vector.tensor_copy(x_grouped[e][:, :, t], x_raw[:, t, :].indirect(offsets[:, e * LC:(e + 1) * LC]))
+            nc.vector.tensor_copy(picked[e][:, t, :], planes[t][:].indirect(offsets[:, e * LC:(e + 1) * LC]))
+
+        def group_x(e):
+            nc.vector.tensor_copy(out=x_grouped[e][:], in_=picked[e][:].rearrange("p t c -> p c t"))
 
         def group_w(e, lo, hi):
             nc.scalar.copy(out=w_grouped[e][:, lo:hi, :], in_=w_raw[e][:, :, lo:hi].rearrange("p j n -> p n j"))
@@ -84,6 +90,7 @@ def tile_routed_moe_kernel(tc, xT, w, gate, offs, out):
 
         for t in range(PACK):
             gather(0, t)
+        group_x(0)
         gather(1, 0)
         quant_x(0)
         group_w(0, 0, P)
@@ -98,6 +105,7 @@ def tile_routed_moe_kernel(tc, xT, w, gate, offs, out):
         empty(0, 1)
         for t in range(1, PACK):
             gather(1, t)
+        group_x(1)
         scatter(0, 0)
         quant_x(1)
         multiply(1, 0)

@@ -12,6 +12,7 @@ U16 = mybir.dt.uint16
 U8 = mybir.dt.uint8
 FP8X4 = mybir.dt.float8_e4m3fn_x4
 MULT = mybir.AluOpType.mult
+COPY = mybir.ActivationFunctionType.Copy
 
 P = 128
 PACK = 4
@@ -34,7 +35,6 @@ def tile_routed_moe_kernel(tc, xT, w, gate, offs, out):
             plane = keep.tile([P, T], F32, name="plane%d" % t)
             nc.sync.dma_start(plane[:], x_view[:, t, :])
             planes.append(plane)
-        picked = [keep.tile([P, PACK, C], F32, name="picked%d" % e) for e in range(E)]
 
         w_raw = []
         for e in range(E):
@@ -48,6 +48,8 @@ def tile_routed_moe_kernel(tc, xT, w, gate, offs, out):
             nc.sync.dma_start(g[:], gate[f * P:(f + 1) * P, :])
             gates.append(g)
 
+        x_bf = keep.tile([P, PACK, T], BF16, name="x_bf")
+        picked = keep.tile([P, PACK, C], F32, name="picked")
         x_grouped = [keep.tile([P, C, PACK], BF16, name="x_grouped%d" % e, align_bytes=64) for e in range(E)]
         x_codes = [keep.tile([P, C], U32, name="x_codes%d" % e, align_bytes=64) for e in range(E)]
         x_scales = [keep.tile([P, C], U8, name="x_scales%d" % e, align_bytes=64) for e in range(E)]
@@ -58,22 +60,19 @@ def tile_routed_moe_kernel(tc, xT, w, gate, offs, out):
         sums = [[keep.tile([P, C], F32, name="sums%d_%d" % (e, f)) for f in range(FB)] for e in range(E)]
         windows = [keep.tile([P, T], F32, name="window%d" % f) for f in range(FB)]
 
-        def gather(e, t):
-            nc.vector.tensor_copy(picked[e][:, t, :], planes[t][:].indirect(offsets[:, e * LC:(e + 1) * LC]))
+        def list_of(e):
+            return offsets[:, e * LC:(e + 1) * LC]
 
-        def group_x(e):
-            nc.vector.tensor_copy(out=x_grouped[e][:], in_=picked[e][:].rearrange("p t c -> p c t"))
-
-        def group_w(e, lo, hi):
-            nc.scalar.copy(out=w_grouped[e][:, lo:hi, :], in_=w_raw[e][:, :, lo:hi].rearrange("p j n -> p n j"))
+        def group_w(e):
+            nc.vector.tensor_copy(out=w_grouped[e][:], in_=w_raw[e][:].rearrange("p j n -> p n j"))
 
         def quant_x(e):
             nc.vector.quantize_mx(out=x_codes[e][:].bitcast(FP8X4), scales=x_scales[e][:],
                                   in_=x_grouped[e][:].rearrange("p c t -> p (c t)"))
 
-        def quant_w(e, lo, hi):
-            nc.vector.quantize_mx(out=w_codes[e][:, lo:hi].bitcast(FP8X4), scales=w_scales[e][:, lo:hi],
-                                  in_=w_grouped[e][:, lo:hi, :].rearrange("p n j -> p (n j)"))
+        def quant_w(e):
+            nc.vector.quantize_mx(out=w_codes[e][:].bitcast(FP8X4), scales=w_scales[e][:],
+                                  in_=w_grouped[e][:].rearrange("p n j -> p (n j)"))
 
         def multiply(e, f):
             cols = slice(f * P, (f + 1) * P)
@@ -81,37 +80,32 @@ def tile_routed_moe_kernel(tc, xT, w, gate, offs, out):
                                 lhsT_scale=w_scales[e][:, cols], rhs=x_codes[e][:].bitcast(FP8X4),
                                 rhs_scale=x_scales[e][:], start=True, stop=True)
 
-        def empty(e, f):
-            nc.scalar.copy(out=sums[e][f][:], in_=acc[e][f][:])
-
         def scatter(e, f):
-            nc.vector.tensor_tensor(windows[f][:].indirect(offsets[:, e * LC:(e + 1) * LC]),
+            nc.vector.tensor_tensor(windows[f][:].indirect(list_of(e)),
                                     sums[e][f][:], gates[f][:, e * C:(e + 1) * C], MULT)
 
         for t in range(PACK):
-            gather(0, t)
-        group_x(0)
-        gather(1, 0)
+            nc.scalar.copy(out=x_bf[:, t, :], in_=planes[t][:])
+        for t in range(PACK):
+            nc.vector.tensor_copy(picked[:, t, :], planes[t][:].indirect(list_of(0)))
+        for t in range(PACK):
+            nc.scalar.activation(x_grouped[1][:, :, t], x_bf[:, t, :].indirect(list_of(1)), COPY)
+        nc.vector.tensor_copy(out=x_grouped[0][:], in_=picked[:].rearrange("p t c -> p c t"))
+        group_w(0)
         quant_x(0)
-        group_w(0, 0, P)
-        quant_w(0, 0, P)
+        quant_w(0)
         multiply(0, 0)
-        group_w(0, P, N)
-        quant_w(0, P, N)
         multiply(0, 1)
-        empty(0, 0)
-        group_w(1, 0, N)
-        quant_w(1, 0, N)
-        empty(0, 1)
-        for t in range(1, PACK):
-            gather(1, t)
-        group_x(1)
+        group_w(1)
+        nc.vector.tensor_copy(out=sums[0][0][:], in_=acc[0][0][:])
+        quant_w(1)
+        nc.vector.tensor_copy(out=sums[0][1][:], in_=acc[0][1][:])
         scatter(0, 0)
         quant_x(1)
         multiply(1, 0)
         multiply(1, 1)
-        empty(1, 0)
-        empty(1, 1)
+        nc.scalar.copy(out=sums[1][0][:], in_=acc[1][0][:])
+        nc.scalar.copy(out=sums[1][1][:], in_=acc[1][1][:])
         scatter(0, 1)
         scatter(1, 0)
         nc.sync.dma_start(out[0:P, :], windows[0][:])

@@ -63,16 +63,16 @@ def tile_routed_moe_kernel(tc, xT, w, gate, offs, out):
         def list_of(e):
             return offsets[:, e * LC:(e + 1) * LC]
 
-        def group_w(e):
-            nc.vector.tensor_copy(out=w_grouped[e][:], in_=w_raw[e][:].rearrange("p j n -> p n j"))
+        def group_w(engine_copy, e, lo, hi):
+            engine_copy(out=w_grouped[e][:, lo:hi, :], in_=w_raw[e][:, :, lo:hi].rearrange("p j n -> p n j"))
 
         def quant_x(e):
             nc.vector.quantize_mx(out=x_codes[e][:].bitcast(FP8X4), scales=x_scales[e][:],
                                   in_=x_grouped[e][:].rearrange("p c t -> p (c t)"))
 
-        def quant_w(e):
-            nc.vector.quantize_mx(out=w_codes[e][:].bitcast(FP8X4), scales=w_scales[e][:],
-                                  in_=w_grouped[e][:].rearrange("p n j -> p (n j)"))
+        def quant_w(e, lo, hi):
+            nc.vector.quantize_mx(out=w_codes[e][:, lo:hi].bitcast(FP8X4), scales=w_scales[e][:, lo:hi],
+                                  in_=w_grouped[e][:, lo:hi, :].rearrange("p n j -> p (n j)"))
 
         def multiply(e, f):
             cols = slice(f * P, (f + 1) * P)
@@ -84,26 +84,29 @@ def tile_routed_moe_kernel(tc, xT, w, gate, offs, out):
             nc.vector.tensor_tensor(windows[f][:].indirect(list_of(e)),
                                     sums[e][f][:], gates[f][:, e * C:(e + 1) * C], MULT)
 
-        for t in range(PACK):
+        for t in range(PACK - 1):
             nc.scalar.copy(out=x_bf[:, t, :], in_=planes[t][:])
         for t in range(PACK):
             nc.vector.tensor_copy(picked[:, t, :], planes[t][:].indirect(list_of(0)))
+        nc.vector.tensor_copy(out=x_bf[:, PACK - 1, :], in_=planes[PACK - 1][:])
         for t in range(PACK):
             nc.scalar.activation(x_grouped[1][:, :, t], x_bf[:, t, :].indirect(list_of(1)), COPY)
         nc.vector.tensor_copy(out=x_grouped[0][:], in_=picked[:].rearrange("p t c -> p c t"))
-        group_w(0)
+        group_w(nc.vector.tensor_copy, 0, 0, P)
         quant_x(0)
-        quant_w(0)
+        quant_w(0, 0, P)
         multiply(0, 0)
+        group_w(nc.vector.tensor_copy, 0, P, N)
+        group_w(nc.vector.tensor_copy, 1, 0, N)
+        quant_w(0, P, N)
         multiply(0, 1)
-        group_w(1)
-        nc.vector.tensor_copy(out=sums[0][0][:], in_=acc[0][0][:])
-        quant_w(1)
-        nc.vector.tensor_copy(out=sums[0][1][:], in_=acc[0][1][:])
-        scatter(0, 0)
+        quant_w(1, 0, N)
+        nc.scalar.copy(out=sums[0][0][:], in_=acc[0][0][:])
+        nc.scalar.copy(out=sums[0][1][:], in_=acc[0][1][:])
         quant_x(1)
         multiply(1, 0)
         multiply(1, 1)
+        scatter(0, 0)
         nc.scalar.copy(out=sums[1][0][:], in_=acc[1][0][:])
         nc.scalar.copy(out=sums[1][1][:], in_=acc[1][1][:])
         scatter(0, 1)

@@ -39,7 +39,12 @@ def tile_routed_moe_kernel(tc, xT, w, gate, offs, out):
         w_raw = []
         for e in range(E):
             raw = keep.tile([P, PACK, N], F32, name="w_raw%d" % e)
-            nc.sync.dma_start(raw[:], w[e].rearrange("(p j) n -> p j n", j=PACK))
+            w_view = w[e].rearrange("(p j) n -> p j n", j=PACK)
+            if e == 0:
+                nc.sync.dma_start(raw[:, :, 0:P], w_view[:, :, 0:P])
+                nc.sync.dma_start(raw[:, :, P:N], w_view[:, :, P:N])
+            else:
+                nc.sync.dma_start(raw[:], w_view)
             w_raw.append(raw)
 
         gates = []
@@ -91,10 +96,10 @@ def tile_routed_moe_kernel(tc, xT, w, gate, offs, out):
         nc.vector.tensor_copy(out=x_bf[:, PACK - 1, :], in_=planes[PACK - 1][:])
         for t in range(PACK):
             nc.scalar.activation(x_grouped[1][:, :, t], x_bf[:, t, :].indirect(list_of(1)), COPY)
-        nc.vector.tensor_copy(out=x_grouped[0][:], in_=picked[:].rearrange("p t c -> p c t"))
         group_w(nc.vector.tensor_copy, 0, 0, P)
-        quant_x(0)
+        nc.vector.tensor_copy(out=x_grouped[0][:], in_=picked[:].rearrange("p t c -> p c t"))
         quant_w(0, 0, P)
+        quant_x(0)
         multiply(0, 0)
         group_w(nc.vector.tensor_copy, 0, P, N)
         group_w(nc.vector.tensor_copy, 1, 0, N)

@@ -26,6 +26,11 @@ def tile_routed_moe_kernel(tc, xT, w, gate, offs, out):
         keep = ctx.enter_context(tc.tile_pool(name="keep", bufs=1))
         psum = ctx.enter_context(tc.psum_pool(name="psum", bufs=1))
 
+        one = keep.tile([P, 1], F32, name="one")
+        one_copy = keep.tile([P, 1], F32, name="one_copy")
+        nc.gpsimd.memset(one[:], 0.0)
+        nc.scalar.activation(one_copy[:], one[:], COPY)
+
         offsets = keep.tile([P, E * C // 16], U16, name="offsets")
         nc.sync.dma_start(offsets[:], offs)
 
@@ -89,11 +94,10 @@ def tile_routed_moe_kernel(tc, xT, w, gate, offs, out):
             nc.vector.tensor_tensor(windows[f][:].indirect(list_of(e)),
                                     sums[e][f][:], gates[f][:, e * C:(e + 1) * C], MULT)
 
-        for t in range(PACK - 1):
-            nc.scalar.copy(out=x_bf[:, t, :], in_=planes[t][:])
+        for t in range(PACK):
+            nc.gpsimd.tensor_copy(out=x_bf[:, t, :], in_=planes[t][:])
         for t in range(PACK):
             nc.vector.tensor_copy(picked[:, t, :], planes[t][:].indirect(list_of(0)))
-        nc.vector.tensor_copy(out=x_bf[:, PACK - 1, :], in_=planes[PACK - 1][:])
         for t in range(PACK):
             nc.scalar.activation(x_grouped[1][:, :, t], x_bf[:, t, :].indirect(list_of(1)), COPY)
         group_w(nc.vector.tensor_copy, 0, 0, P)

@@ -18,6 +18,7 @@ P = 128
 PACK = 4
 FB = N // P
 LC = C // 16
+RUN = 4
 
 
 def tile_routed_moe_kernel(tc, xT, w, gate, offs, out):
@@ -74,7 +75,8 @@ def tile_routed_moe_kernel(tc, xT, w, gate, offs, out):
             return offsets[:, e * LC:(e + 1) * LC]
 
         def group_w(engine_copy, e, lo, hi):
-            engine_copy(out=w_grouped[e][:, lo:hi, :], in_=w_raw[e][:, :, lo:hi].rearrange("p j n -> p n j"))
+            engine_copy(out=w_grouped[e][:, lo:hi, :].rearrange("p (c i) j -> p c j i", i=RUN),
+                        in_=w_raw[e][:, :, lo:hi].rearrange("p j (c i) -> p c j i", i=RUN))
 
         def quant_x(e):
             nc.vector.quantize_mx(out=x_codes[e][:].bitcast(FP8X4), scales=x_scales[e][:],
@@ -101,7 +103,8 @@ def tile_routed_moe_kernel(tc, xT, w, gate, offs, out):
         for t in range(PACK):
             nc.scalar.activation(x_grouped[1][:, :, t], x_bf[:, t, :].indirect(list_of(1)), COPY)
         group_w(nc.vector.tensor_copy, 0, 0, P)
-        nc.vector.tensor_copy(out=x_grouped[0][:], in_=picked[:].rearrange("p t c -> p c t"))
+        nc.vector.tensor_copy(out=x_grouped[0][:].rearrange("p (c i) t -> p c t i", i=RUN),
+                              in_=picked[:].rearrange("p t (c i) -> p c t i", i=RUN))
         quant_w(0, 0, P)
         quant_x(0)
         multiply(0, 0)

@@ -18,7 +18,7 @@ P = 128
 PACK = 4
 FB = N // P
 LC = C // 16
-RUN = 4
+RUN = 8
 
 
 def tile_routed_moe_kernel(tc, xT, w, gate, offs, out):

from contextlib import ExitStack

import concourse.mybir as mybir

K, T, E, C, N = 512, 512, 2, 256, 256
FLOPS = 2 * K * N * E * C

F32 = mybir.dt.float32
BF16 = mybir.dt.bfloat16
U32 = mybir.dt.uint32
U16 = mybir.dt.uint16
U8 = mybir.dt.uint8
FP8X4 = mybir.dt.float8_e4m3fn_x4
MULT = mybir.AluOpType.mult
COPY = mybir.ActivationFunctionType.Copy

P = 128
PACK = 4
FB = N // P
LC = C // 16
RUN = 8


def tile_routed_moe_kernel(tc, xT, w, gate, offs, out):
    nc = tc.nc
    with ExitStack() as ctx:
        keep = ctx.enter_context(tc.tile_pool(name="keep", bufs=1))
        psum = ctx.enter_context(tc.psum_pool(name="psum", bufs=1))

        one = keep.tile([P, 1], F32, name="one")
        one_copy = keep.tile([P, 1], F32, name="one_copy")
        nc.gpsimd.memset(one[:], 0.0)
        nc.scalar.activation(one_copy[:], one[:], COPY)

        offsets = keep.tile([P, E * C // 16], U16, name="offsets")
        nc.sync.dma_start(offsets[:], offs)

        x_view = xT.rearrange("(p t) n -> p t n", t=PACK)
        planes = []
        for t in range(PACK):
            plane = keep.tile([P, T], F32, name="plane%d" % t)
            nc.sync.dma_start(plane[:], x_view[:, t, :])
            planes.append(plane)

        w_raw = []
        for e in range(E):
            raw = keep.tile([P, PACK, N], F32, name="w_raw%d" % e)
            w_view = w[e].rearrange("(p j) n -> p j n", j=PACK)
            if e == 0:
                nc.sync.dma_start(raw[:, :, 0:P], w_view[:, :, 0:P])
                nc.sync.dma_start(raw[:, :, P:N], w_view[:, :, P:N])
            else:
                nc.sync.dma_start(raw[:], w_view)
            w_raw.append(raw)

        gates = []
        for f in range(FB):
            g = keep.tile([P, E * C], F32, name="gate%d" % f)
            nc.sync.dma_start(g[:], gate[f * P:(f + 1) * P, :])
            gates.append(g)

        x_bf = keep.tile([P, PACK, T], BF16, name="x_bf")
        picked = keep.tile([P, PACK, C], F32, name="picked")
        x_grouped = [keep.tile([P, C, PACK], BF16, name="x_grouped%d" % e, align_bytes=64) for e in range(E)]
        x_codes = [keep.tile([P, C], U32, name="x_codes%d" % e, align_bytes=64) for e in range(E)]
        x_scales = [keep.tile([P, C], U8, name="x_scales%d" % e, align_bytes=64) for e in range(E)]
        w_grouped = [keep.tile([P, N, PACK], BF16, name="w_grouped%d" % e, align_bytes=64) for e in range(E)]
        w_codes = [keep.tile([P, N], U32, name="w_codes%d" % e, align_bytes=64) for e in range(E)]
        w_scales = [keep.tile([P, N], U8, name="w_scales%d" % e, align_bytes=64) for e in range(E)]
        acc = [[psum.tile([P, C], F32, name="acc%d_%d" % (e, f)) for f in range(FB)] for e in range(E)]
        sums = [[keep.tile([P, C], F32, name="sums%d_%d" % (e, f)) for f in range(FB)] for e in range(E)]
        windows = [keep.tile([P, T], F32, name="window%d" % f) for f in range(FB)]

        def list_of(e):
            return offsets[:, e * LC:(e + 1) * LC]

        def group_w(engine_copy, e, lo, hi):
            engine_copy(out=w_grouped[e][:, lo:hi, :].rearrange("p (c i) j -> p c j i", i=RUN),
                        in_=w_raw[e][:, :, lo:hi].rearrange("p j (c i) -> p c j i", i=RUN))

        def quant_x(e):
            nc.vector.quantize_mx(out=x_codes[e][:].bitcast(FP8X4), scales=x_scales[e][:],
                                  in_=x_grouped[e][:].rearrange("p c t -> p (c t)"))

        def quant_w(e, lo, hi):
            nc.vector.quantize_mx(out=w_codes[e][:, lo:hi].bitcast(FP8X4), scales=w_scales[e][:, lo:hi],
                                  in_=w_grouped[e][:, lo:hi, :].rearrange("p n j -> p (n j)"))

        def multiply(e, f):
            cols = slice(f * P, (f + 1) * P)
            nc.tensor.matmul_mx(out=acc[e][f][:], lhsT=w_codes[e][:, cols].bitcast(FP8X4),
                                lhsT_scale=w_scales[e][:, cols], rhs=x_codes[e][:].bitcast(FP8X4),
                                rhs_scale=x_scales[e][:], start=True, stop=True)

        def scatter(e, f):
            nc.vector.tensor_tensor(windows[f][:].indirect(list_of(e)),
                                    sums[e][f][:], gates[f][:, e * C:(e + 1) * C], MULT)

        for t in range(PACK):
            nc.gpsimd.tensor_copy(out=x_bf[:, t, :], in_=planes[t][:])
        for t in range(PACK):
            nc.vector.tensor_copy(picked[:, t, :], planes[t][:].indirect(list_of(0)))
        for t in range(PACK):
            nc.scalar.activation(x_grouped[1][:, :, t], x_bf[:, t, :].indirect(list_of(1)), COPY)
        group_w(nc.vector.tensor_copy, 0, 0, P)
        nc.vector.tensor_copy(out=x_grouped[0][:].rearrange("p (c i) t -> p c t i", i=RUN),
                              in_=picked[:].rearrange("p t (c i) -> p c t i", i=RUN))
        quant_w(0, 0, P)
        quant_x(0)
        multiply(0, 0)
        group_w(nc.vector.tensor_copy, 0, P, N)
        group_w(nc.vector.tensor_copy, 1, 0, N)
        quant_w(0, P, N)
        multiply(0, 1)
        quant_w(1, 0, N)
        nc.scalar.copy(out=sums[0][0][:], in_=acc[0][0][:])
        nc.scalar.copy(out=sums[0][1][:], in_=acc[0][1][:])
        quant_x(1)
        multiply(1, 0)
        multiply(1, 1)
        scatter(0, 0)
        nc.scalar.copy(out=sums[1][0][:], in_=acc[1][0][:])
        nc.scalar.copy(out=sums[1][1][:], in_=acc[1][1][:])
        scatter(0, 1)
        scatter(1, 0)
        nc.sync.dma_start(out[0:P, :], windows[0][:])
        scatter(1, 1)
        nc.sync.dma_start(out[P:2 * P, :], windows[1][:])
